import numpy as np
import ml_dtypes


def mxq(x, axis, fmt="e4m3"):
    dtype, down = {"e4m3": (ml_dtypes.float8_e4m3fn, 7), "e5m2": (ml_dtypes.float8_e5m2, 14)}[fmt]
    v = np.moveaxis(np.asarray(x, np.float32).astype(ml_dtypes.bfloat16).astype(np.float64), axis, -1)
    blocks = v.reshape(v.shape[:-1] + (-1, 32))
    amax = np.abs(blocks).max(-1, keepdims=True)
    byte = np.maximum(np.where(amax > 0, np.frexp(amax)[1] - 1 + 127, 0) - down, 1)
    scale = np.exp2(byte - 127.0)
    codes = (blocks / scale).astype(np.float32).astype(dtype).astype(np.float64)
    return np.moveaxis((codes * scale).reshape(v.shape), -1, axis)


WIDE = False


def mx_kscale(k):
    if not WIDE:
        return np.ones(k)
    levels = np.array([10, -10, 5, -5, 0])
    if k % 512:
        return np.exp2(np.random.permutation(np.resize(levels, k // 32))).repeat(32)
    a = np.empty((k // 512, 16))
    for p in range(k // 512):
        a[p, :8] = np.random.permutation(np.resize(levels, 8))
        for g in range(8):
            far = levels[np.abs(levels - a[p, g]) >= 10]
            a[p, g + 8] = far[np.random.randint(len(far))]
    return np.exp2(a.ravel()).repeat(32)


def f64(x):
    return np.asarray(x).astype(np.float64)


def striped(idx):
    return np.tile(idx.reshape(-1, 16).T, (8, 1)).astype(np.uint16)


def unstriped(offs):
    return offs[:16].T.reshape(-1).astype(np.int64)


def pack_weight(w):
    k, n = w.shape
    w = f64(np.asarray(w, np.float32).astype(ml_dtypes.bfloat16)).reshape(k // 32, 32, n)
    amax = np.abs(w).max(1)
    byte = np.clip(np.where(amax > 0, np.frexp(amax)[1] - 1 + 127 - 7, 1), 1, 254)
    scaled = (w * np.exp2(127.0 - byte)[:, None, :]).reshape(k, n).astype(np.float32)
    words = np.ascontiguousarray(scaled.reshape(k // 512, 128, 4, n).transpose(0, 1, 3, 2)).astype(ml_dtypes.float8_e4m3fn).view(np.uint8)
    return words, np.ascontiguousarray(byte.astype(np.uint8).reshape(k // 512, 16, n))


def unpack_weight(words, scales):
    g, p, n, _ = words.shape
    vals = np.ascontiguousarray(words).view(ml_dtypes.float8_e4m3fn).astype(np.float64) * np.repeat(np.exp2(scales.astype(np.float64) - 127.0), 8, axis=1)[..., None]
    return vals.transpose(0, 1, 3, 2).reshape(g * 512, n)


K, T, S, N = 512, 2048, 512, 128
P = 2 ** 7


def setup_inputs():
    n = np.random.standard_normal
    s = mx_kscale(K)[:, None]
    packed_xT = pack_weight(n((K, T)) * s)
    return {
        "x_words": packed_xT[0],
        "x_scales": packed_xT[1],
        "w1": (n((K, N)) / np.sqrt(K) / s).astype(np.float32),
        "fe": (n((N, S))).astype(np.float32),
        "fh": (n((N, S))).astype(np.float32),
        "ca": (np.tile(np.random.uniform(0.5, 0.95, S), (P, 1))).astype(np.float32),
        "cur": (n((N, S))).astype(np.float32),
        "wp2": (np.random.uniform(0.2, 0.8, (N, 1))).astype(np.float32),
        "da": (np.tile(np.random.uniform(0.6, 1.0, S), (P, 1))).astype(np.float32),
        "offs": striped(np.random.permutation(T)[:S]),
        "up": striped(np.random.permutation(S)),
        "dn": striped(np.random.permutation(S)),
        "lt": striped(np.random.permutation(S)),
        "rt": striped(np.random.permutation(S)),
    }


def reference(x_words, x_scales, w1, fe, fh, ca, cur, wp2, da, offs, up, dn, lt, rt):
    curl = f64(fh)[:, unstriped(up)] - f64(fh)[:, unstriped(dn)]
    jn = 0.7 * f64(cur) + f64(wp2) * f64(fe)
    xq = unpack_weight(x_words, x_scales)[:, unstriped(offs)]
    y = mxq(f64(w1), 0, "e4m3").T @ xq
    en = f64(fe) * f64(ca)[:1] + 0.5 * curl - (0.6 * jn) - (0.4 * y)
    return f64(fh) * f64(da)[:1] + 0.5 * (en[:, unstriped(lt)] - en[:, unstriped(rt)])

@@ -1,0 +1,127 @@
+from contextlib import ExitStack
+
+import concourse.mybir as mybir
+
+K, T, S, N = 512, 2048, 512, 128
+P = 128
+FLOPS = 2 * K * N * S
+
+F32 = mybir.dt.float32
+BF16 = mybir.dt.bfloat16
+I32 = mybir.dt.int32
+U32 = mybir.dt.uint32
+U16 = mybir.dt.uint16
+U8 = mybir.dt.uint8
+FP8X4 = mybir.dt.float8_e4m3fn_x4
+MULT = mybir.AluOpType.mult
+ADD = mybir.AluOpType.add
+SUB = mybir.AluOpType.subtract
+IDENT = mybir.ActivationFunctionType.Identity
+HALF = S // 2
+
+
+def tile_picked_yfdtd_drude_p_kernel(
+    tc, x_words, x_scales, w1, fe, fh, ca, cur, wp2, da, offs, up, dn, lt, rt, out
+):
+    nc = tc.nc
+    with ExitStack() as ctx:
+        lists = ctx.enter_context(tc.tile_pool(name="lists", bufs=1))
+        sb = ctx.enter_context(tc.tile_pool(name="sb", bufs=1))
+        ps = ctx.enter_context(tc.psum_pool(name="ps", bufs=1))
+
+        def f32_tile(name):
+            return sb.tile([P, S], F32, name=name, align_bytes=64)
+
+        def list_tile(name):
+            return lists.tile([P, S // 16], U16, name=name)
+
+        def cols(h):
+            return slice(h * HALF, (h + 1) * HALF)
+
+        def lcols(h):
+            return slice(h * HALF // 16, (h + 1) * HALF // 16)
+
+        fh_t, fe_t, ca_t, cur_t, da_t = [f32_tile(n) for n in ("fh", "fe", "ca", "cur", "da")]
+        offs_t, up_t, dn_t, lt_t, rt_t = [list_tile(n) for n in ("offs", "up", "dn", "lt", "rt")]
+        words = sb.tile([P, T], U32, name="words", align_bytes=64)
+        scales = sb.tile([P, T], U8, name="scales", align_bytes=64)
+        w_raw = sb.tile([P, 4, N], F32, name="w_raw", align_bytes=64)
+        wp_t = sb.tile([P, 1], F32, name="wp")
+
+        nc.vector.memset(scales[:].bitcast(I32), 0)
+        nc.sync.dma_start(out=fh_t[:], in_=fh)
+        nc.sync.dma_start(up_t[:], up)
+        nc.sync.dma_start(dn_t[:], dn)
+        nc.sync.dma_start(offs_t[:], offs)
+        for q in range(4):
+            nc.scalar.dma_start(
+                out=scales[32 * q : 32 * q + 4, :].bitcast(I32),
+                in_=x_scales[0, 4 * q : 4 * q + 4, :].bitcast(I32),
+            )
+        nc.sync.dma_start(
+            out=words[:].bitcast(I32),
+            in_=x_words[0].rearrange("p n t -> p (n t)").bitcast(I32),
+        )
+        nc.sync.dma_start(out=w_raw[:], in_=w1.rearrange("(p j) n -> p j n", j=4))
+        nc.scalar.dma_start(out=wp_t[:], in_=wp2)
+        nc.sync.dma_start(out=fe_t[:], in_=fe)
+        nc.sync.dma_start(out=ca_t[:], in_=ca)
+        nc.sync.dma_start(out=cur_t[:], in_=cur)
+        nc.sync.dma_start(out=da_t[:], in_=da)
+        nc.sync.dma_start(rt_t[:], rt)
+        nc.sync.dma_start(lt_t[:], lt)
+
+        u = f32_tile("u")
+        c = f32_tile("c")
+        for h in range(2):
+            nc.vector.tensor_copy(u[:, cols(h)], fh_t[:].indirect(up_t[:, lcols(h)]))
+        for h in range(2):
+            nc.vector.tensor_tensor(c[:, cols(h)], fh_t[:].indirect(dn_t[:, lcols(h)]), u[:, cols(h)], SUB)
+
+        g_scales = sb.tile([P, S], U8, name="g_scales", align_bytes=64)
+        g_words = sb.tile([P, S], U32, name="g_words", align_bytes=64)
+        nc.vector.tensor_copy(g_scales[:], scales[:].indirect(offs_t[:]))
+        nc.vector.tensor_copy(g_words[:], words[:].indirect(offs_t[:]))
+
+        w_bf = sb.tile([P, N, 4], BF16, name="w_bf", align_bytes=64)
+        nc.scalar.copy(out=w_bf[:], in_=w_raw[:].rearrange("p j n -> p n j"))
+        w_codes = sb.tile([P, N], U32, name="w_codes", align_bytes=64)
+        w_scales = sb.tile([P, N], U8, name="w_scales", align_bytes=64)
+        nc.vector.quantize_mx(
+            out=w_codes[:].bitcast(FP8X4),
+            scales=w_scales[:],
+            in_=w_bf[:].rearrange("p n j -> p (n j)"),
+        )
+        y = ps.tile([P, S], F32, name="y")
+        nc.tensor.matmul_mx(
+            out=y[:],
+            lhsT=w_codes[:].bitcast(FP8X4),
+            lhsT_scale=w_scales[:],
+            rhs=g_words[:].bitcast(FP8X4),
+            rhs_scale=g_scales[:],
+            start=True,
+            stop=True,
+        )
+
+        wpn = sb.tile([P, 1], F32, name="wpn")
+        nc.scalar.mul(wpn[:], wp_t[:], -0.3)
+        a_t = f32_tile("a")
+        nc.scalar.activation(a_t[:], ca_t[:], IDENT, bias=wpn[:], scale=0.5)
+        x0 = f32_tile("x0")
+        p1 = f32_tile("p1")
+        p2 = f32_tile("p2")
+        d_t = f32_tile("d")
+        e_t = f32_tile("e")
+        nc.vector.tensor_tensor(x0[:], fe_t[:], a_t[:], MULT)
+        nc.vector.scalar_tensor_tensor(p1[:], c[:], -0.25, x0[:], MULT, ADD)
+        nc.vector.tensor_tensor(d_t[:], fh_t[:], da_t[:], MULT)
+        nc.vector.scalar_tensor_tensor(p2[:], cur_t[:], -0.21, p1[:], MULT, ADD)
+        nc.vector.scalar_tensor_tensor(e_t[:], y[:], -0.2, p2[:], MULT, ADD)
+
+        r_t = f32_tile("r")
+        o_t = f32_tile("o")
+        for h in range(2):
+            nc.vector.tensor_tensor(r_t[:, cols(h)], e_t[:].indirect(rt_t[:, lcols(h)]), d_t[:, cols(h)], SUB)
+        for h in range(2):
+            nc.vector.tensor_tensor(o_t[:, cols(h)], e_t[:].indirect(lt_t[:, lcols(h)]), r_t[:, cols(h)], SUB)
+            nc.sync.dma_start(out=out[:, cols(h)], in_=o_t[:, cols(h)])

@@ -1,6 +1,7 @@
 from contextlib import ExitStack
 
 import concourse.mybir as mybir
+from concourse.masks import make_identity
 
 K, T, S, N = 512, 2048, 512, 128
 P = 128
@@ -17,7 +18,9 @@ MULT = mybir.AluOpType.mult
 ADD = mybir.AluOpType.add
 SUB = mybir.AluOpType.subtract
 IDENT = mybir.ActivationFunctionType.Identity
+COPY = mybir.ActivationFunctionType.Copy
 HALF = S // 2
+BLOCKS = S // P
 
 
 def tile_picked_yfdtd_drude_p_kernel(
@@ -41,50 +44,99 @@ def tile_picked_yfdtd_drude_p_kernel(
         def lcols(h):
             return slice(h * HALF // 16, (h + 1) * HALF // 16)
 
-        fh_t, fe_t, ca_t, cur_t, da_t = [f32_tile(n) for n in ("fh", "fe", "ca", "cur", "da")]
+        def blk(t):
+            return slice(t * P, (t + 1) * P)
+
+        fh_t, fe_t, cur_t, da_t = [f32_tile(n) for n in ("fh", "fe", "cur", "da")]
         offs_t, up_t, dn_t, lt_t, rt_t = [list_tile(n) for n in ("offs", "up", "dn", "lt", "rt")]
         words = sb.tile([P, T], U32, name="words", align_bytes=64)
-        scales = sb.tile([P, T], U8, name="scales", align_bytes=64)
-        w_raw = sb.tile([P, 4, N], F32, name="w_raw", align_bytes=64)
+        scales = sb.tile([P, T], U8, name="scales", tag="scales_then_words", align_bytes=64)
+        w_raw = sb.tile([P, 4, N], F32, name="w_raw", tag="w_then_p", align_bytes=64)
         wp_t = sb.tile([P, 1], F32, name="wp")
+        ca_rows = sb.tile([P, P], F32, name="ca_rows", align_bytes=64)
+        ident = sb.tile([P, P], F32, name="ident", align_bytes=64)
+        warm_in = sb.tile([P, 1], F32, name="warm_in")
+        warm_out = sb.tile([P, 1], F32, name="warm_out")
 
-        nc.vector.memset(scales[:].bitcast(I32), 0)
-        nc.sync.dma_start(out=fh_t[:], in_=fh)
-        nc.sync.dma_start(up_t[:], up)
-        nc.sync.dma_start(dn_t[:], dn)
-        nc.sync.dma_start(offs_t[:], offs)
-        for q in range(4):
-            nc.scalar.dma_start(
+        def load_scales(queue, q):
+            queue.dma_start(
                 out=scales[32 * q : 32 * q + 4, :].bitcast(I32),
                 in_=x_scales[0, 4 * q : 4 * q + 4, :].bitcast(I32),
             )
-        nc.sync.dma_start(
-            out=words[:].bitcast(I32),
-            in_=x_words[0].rearrange("p n t -> p (n t)").bitcast(I32),
-        )
-        nc.sync.dma_start(out=w_raw[:], in_=w1.rearrange("(p j) n -> p j n", j=4))
+
+        def load_words():
+            nc.sync.dma_start(
+                out=words[:].bitcast(I32),
+                in_=x_words[0].rearrange("p n t -> p (n t)").bitcast(I32),
+            )
+
+        nc.vector.memset(warm_in[:], 0.0)
+        nc.scalar.activation(warm_out[:], warm_in[:], IDENT)
+        nc.vector.memset(scales[:].bitcast(I32), 0)
+        make_identity(nc, ident[:])
+        nc.sync.dma_start(up_t[:], up)
         nc.scalar.dma_start(out=wp_t[:], in_=wp2)
+        nc.sync.dma_start(out=fh_t[:], in_=fh)
+        nc.sync.dma_start(dn_t[:], dn)
+        nc.sync.dma_start(offs_t[:], offs)
+        nc.sync.dma_start(out=ca_rows[:], in_=ca[0:32, :].rearrange("a (t c) -> (a t) c", c=P))
         nc.sync.dma_start(out=fe_t[:], in_=fe)
-        nc.sync.dma_start(out=ca_t[:], in_=ca)
         nc.sync.dma_start(out=cur_t[:], in_=cur)
+        load_words()
+        nc.sync.dma_start(out=w_raw[:], in_=w1.rearrange("(p j) n -> p j n", j=4))
         nc.sync.dma_start(out=da_t[:], in_=da)
         nc.sync.dma_start(rt_t[:], rt)
         nc.sync.dma_start(lt_t[:], lt)
+        for q in range(4):
+            load_scales(nc.scalar, q)
 
         u = f32_tile("u")
-        c = f32_tile("c")
+        c = sb.tile([P, S], F32, name="c", tag="c_w_d", align_bytes=64)
         for h in range(2):
             nc.vector.tensor_copy(u[:, cols(h)], fh_t[:].indirect(up_t[:, lcols(h)]))
         for h in range(2):
             nc.vector.tensor_tensor(c[:, cols(h)], fh_t[:].indirect(dn_t[:, lcols(h)]), u[:, cols(h)], SUB)
 
         g_scales = sb.tile([P, S], U8, name="g_scales", align_bytes=64)
-        g_words = sb.tile([P, S], U32, name="g_words", align_bytes=64)
+        g_words = sb.tile([P, S], U32, name="g_words", tag="scales_then_words", align_bytes=64)
         nc.vector.tensor_copy(g_scales[:], scales[:].indirect(offs_t[:]))
         nc.vector.tensor_copy(g_words[:], words[:].indirect(offs_t[:]))
 
-        w_bf = sb.tile([P, N, 4], BF16, name="w_bf", align_bytes=64)
+        wps = sb.tile([P, 1], F32, name="wps")
+        nc.scalar.mul(wps[:], wp_t[:], 1.2)
+        ca_t = ps.tile([P, P], F32, name="ca_t", tag="ca_then_y")
+        nc.tensor.transpose(ca_t[:], ca_rows[:], ident[:])
+        ca_col = sb.tile([P, BLOCKS], F32, name="ca_col")
+        nc.scalar.activation(ca_col[:], ca_t[:, 0:BLOCKS], COPY, scale=0.5)
+
+        fe_tr = ps.tile([P, S], F32, name="fe_tr")
+        for t in range(BLOCKS):
+            nc.tensor.transpose(fe_tr[:, blk(t)], fe_t[:, blk(t)], ident[:])
+        s1 = f32_tile("s1")
+        s2 = f32_tile("s2")
+        z = f32_tile("z")
+        nc.scalar.activation(s1[:], fe_t[:], IDENT, scale=wps[:])
+        for t in range(BLOCKS):
+            nc.scalar.activation(z[:, blk(t)], fe_tr[:, blk(t)], IDENT, scale=ca_col[:, t : t + 1])
+        nc.scalar.activation(s2[:], cur_t[:], COPY, scale=0.84)
+
+        sums = [ps.tile([P, P], F32, name="sum%d" % t) for t in range(BLOCKS)]
+        for i, term in enumerate((s1, s2, c)):
+            for t in range(BLOCKS):
+                nc.tensor.matmul(sums[t][:], term[:, blk(t)], ident[:], start=(i == 0), stop=(i == 2), is_transpose=True)
+        fs = f32_tile("fs")
+        p_ps = ps.tile([P, S], F32, name="p_ps")
+        for t in range(BLOCKS):
+            nc.scalar.activation(fs[:, blk(t)], sums[t][:], COPY, scale=-0.25)
+        for t in range(BLOCKS):
+            nc.tensor.matmul(p_ps[:, blk(t)], z[:, blk(t)], ident[:], start=True, stop=False, is_transpose=True)
+            nc.tensor.matmul(p_ps[:, blk(t)], fs[:, blk(t)], ident[:], start=False, stop=True, is_transpose=True)
+
+        w_bf = sb.tile([P, N, 4], BF16, name="w_bf", tag="c_w_d", align_bytes=64)
         nc.scalar.copy(out=w_bf[:], in_=w_raw[:].rearrange("p j n -> p n j"))
+        p_sb = sb.tile([P, S], F32, name="p_sb", tag="w_then_p", align_bytes=64)
+        nc.scalar.copy(out=p_sb[:], in_=p_ps[:])
+
         w_codes = sb.tile([P, N], U32, name="w_codes", align_bytes=64)
         w_scales = sb.tile([P, N], U8, name="w_scales", align_bytes=64)
         nc.vector.quantize_mx(
@@ -92,31 +144,23 @@ def tile_picked_yfdtd_drude_p_kernel(
             scales=w_scales[:],
             in_=w_bf[:].rearrange("p n j -> p (n j)"),
         )
-        y = ps.tile([P, S], F32, name="y")
-        nc.tensor.matmul_mx(
-            out=y[:],
-            lhsT=w_codes[:].bitcast(FP8X4),
-            lhsT_scale=w_scales[:],
-            rhs=g_words[:].bitcast(FP8X4),
-            rhs_scale=g_scales[:],
-            start=True,
-            stop=True,
-        )
+        ys = [ps.tile([P, HALF], F32, name="y0"), ps.tile([P, HALF], F32, name="y1", tag="ca_then_y")]
+        for h in range(2):
+            nc.tensor.matmul_mx(
+                out=ys[h][:],
+                lhsT=w_codes[:].bitcast(FP8X4),
+                lhsT_scale=w_scales[:],
+                rhs=g_words[:, cols(h)].bitcast(FP8X4),
+                rhs_scale=g_scales[:, cols(h)],
+                start=True,
+                stop=True,
+            )
 
-        wpn = sb.tile([P, 1], F32, name="wpn")
-        nc.scalar.mul(wpn[:], wp_t[:], -0.3)
-        a_t = f32_tile("a")
-        nc.scalar.activation(a_t[:], ca_t[:], IDENT, bias=wpn[:], scale=0.5)
-        x0 = f32_tile("x0")
-        p1 = f32_tile("p1")
-        p2 = f32_tile("p2")
-        d_t = f32_tile("d")
+        d_t = sb.tile([P, S], F32, name="d", tag="c_w_d", align_bytes=64)
         e_t = f32_tile("e")
-        nc.vector.tensor_tensor(x0[:], fe_t[:], a_t[:], MULT)
-        nc.vector.scalar_tensor_tensor(p1[:], c[:], -0.25, x0[:], MULT, ADD)
         nc.vector.tensor_tensor(d_t[:], fh_t[:], da_t[:], MULT)
-        nc.vector.scalar_tensor_tensor(p2[:], cur_t[:], -0.21, p1[:], MULT, ADD)
-        nc.vector.scalar_tensor_tensor(e_t[:], y[:], -0.2, p2[:], MULT, ADD)
+        for h in range(2):
+            nc.vector.scalar_tensor_tensor(e_t[:, cols(h)], ys[h][:], -0.2, p_sb[:, cols(h)], MULT, ADD)
 
         r_t = f32_tile("r")
         o_t = f32_tile("o")

@@ -55,8 +55,6 @@ def tile_picked_yfdtd_drude_p_kernel(
         wp_t = sb.tile([P, 1], F32, name="wp")
         ca_rows = sb.tile([P, P], F32, name="ca_rows", align_bytes=64)
         ident = sb.tile([P, P], F32, name="ident", align_bytes=64)
-        warm_in = sb.tile([P, 1], F32, name="warm_in")
-        warm_out = sb.tile([P, 1], F32, name="warm_out")
 
         def load_scales(queue, q):
             queue.dma_start(
@@ -70,18 +68,16 @@ def tile_picked_yfdtd_drude_p_kernel(
                 in_=x_words[0].rearrange("p n t -> p (n t)").bitcast(I32),
             )
 
-        nc.vector.memset(warm_in[:], 0.0)
-        nc.scalar.activation(warm_out[:], warm_in[:], IDENT)
         nc.vector.memset(scales[:].bitcast(I32), 0)
         make_identity(nc, ident[:])
         nc.sync.dma_start(up_t[:], up)
         nc.scalar.dma_start(out=wp_t[:], in_=wp2)
-        nc.sync.dma_start(out=fh_t[:], in_=fh)
         nc.sync.dma_start(dn_t[:], dn)
-        nc.sync.dma_start(offs_t[:], offs)
+        nc.sync.dma_start(out=fh_t[:], in_=fh)
         nc.sync.dma_start(out=ca_rows[:], in_=ca[0:32, :].rearrange("a (t c) -> (a t) c", c=P))
         nc.sync.dma_start(out=fe_t[:], in_=fe)
         nc.sync.dma_start(out=cur_t[:], in_=cur)
+        nc.sync.dma_start(offs_t[:], offs)
         load_words()
         nc.sync.dma_start(out=w_raw[:], in_=w1.rearrange("(p j) n -> p j n", j=4))
         nc.sync.dma_start(out=da_t[:], in_=da)

from contextlib import ExitStack

import concourse.mybir as mybir
from concourse.masks import make_identity

K, T, S, N = 512, 2048, 512, 128
P = 128
FLOPS = 2 * K * N * S

F32 = mybir.dt.float32
BF16 = mybir.dt.bfloat16
I32 = mybir.dt.int32
U32 = mybir.dt.uint32
U16 = mybir.dt.uint16
U8 = mybir.dt.uint8
FP8X4 = mybir.dt.float8_e4m3fn_x4
MULT = mybir.AluOpType.mult
ADD = mybir.AluOpType.add
SUB = mybir.AluOpType.subtract
IDENT = mybir.ActivationFunctionType.Identity
COPY = mybir.ActivationFunctionType.Copy
HALF = S // 2
BLOCKS = S // P


def tile_picked_yfdtd_drude_p_kernel(
    tc, x_words, x_scales, w1, fe, fh, ca, cur, wp2, da, offs, up, dn, lt, rt, out
):
    nc = tc.nc
    with ExitStack() as ctx:
        lists = ctx.enter_context(tc.tile_pool(name="lists", bufs=1))
        sb = ctx.enter_context(tc.tile_pool(name="sb", bufs=1))
        ps = ctx.enter_context(tc.psum_pool(name="ps", bufs=1))

        def f32_tile(name):
            return sb.tile([P, S], F32, name=name, align_bytes=64)

        def list_tile(name):
            return lists.tile([P, S // 16], U16, name=name)

        def cols(h):
            return slice(h * HALF, (h + 1) * HALF)

        def lcols(h):
            return slice(h * HALF // 16, (h + 1) * HALF // 16)

        def blk(t):
            return slice(t * P, (t + 1) * P)

        fh_t, fe_t, cur_t, da_t = [f32_tile(n) for n in ("fh", "fe", "cur", "da")]
        offs_t, up_t, dn_t, lt_t, rt_t = [list_tile(n) for n in ("offs", "up", "dn", "lt", "rt")]
        words = sb.tile([P, T], U32, name="words", align_bytes=64)
        scales = sb.tile([P, T], U8, name="scales", tag="scales_then_words", align_bytes=64)
        w_raw = sb.tile([P, 4, N], F32, name="w_raw", tag="w_then_p", align_bytes=64)
        wp_t = sb.tile([P, 1], F32, name="wp")
        ca_rows = sb.tile([P, P], F32, name="ca_rows", align_bytes=64)
        ident = sb.tile([P, P], F32, name="ident", align_bytes=64)

        def load_scales(queue, q):
            queue.dma_start(
                out=scales[32 * q : 32 * q + 4, :].bitcast(I32),
                in_=x_scales[0, 4 * q : 4 * q + 4, :].bitcast(I32),
            )

        def load_words():
            nc.sync.dma_start(
                out=words[:].bitcast(I32),
                in_=x_words[0].rearrange("p n t -> p (n t)").bitcast(I32),
            )

        nc.vector.memset(scales[:].bitcast(I32), 0)
        make_identity(nc, ident[:])
        nc.sync.dma_start(up_t[:], up)
        nc.scalar.dma_start(out=wp_t[:], in_=wp2)
        nc.sync.dma_start(dn_t[:], dn)
        nc.sync.dma_start(out=fh_t[:], in_=fh)
        nc.sync.dma_start(out=ca_rows[:], in_=ca[0:32, :].rearrange("a (t c) -> (a t) c", c=P))
        nc.sync.dma_start(out=fe_t[:], in_=fe)
        nc.sync.dma_start(out=cur_t[:], in_=cur)
        nc.sync.dma_start(offs_t[:], offs)
        load_words()
        nc.sync.dma_start(out=w_raw[:], in_=w1.rearrange("(p j) n -> p j n", j=4))
        nc.sync.dma_start(out=da_t[:], in_=da)
        nc.sync.dma_start(rt_t[:], rt)
        nc.sync.dma_start(lt_t[:], lt)
        for q in range(4):
            load_scales(nc.scalar, q)

        u = f32_tile("u")
        c = sb.tile([P, S], F32, name="c", tag="c_w_d", align_bytes=64)
        for h in range(2):
            nc.vector.tensor_copy(u[:, cols(h)], fh_t[:].indirect(up_t[:, lcols(h)]))
        for h in range(2):
            nc.vector.tensor_tensor(c[:, cols(h)], fh_t[:].indirect(dn_t[:, lcols(h)]), u[:, cols(h)], SUB)

        g_scales = sb.tile([P, S], U8, name="g_scales", align_bytes=64)
        g_words = sb.tile([P, S], U32, name="g_words", tag="scales_then_words", align_bytes=64)
        nc.vector.tensor_copy(g_scales[:], scales[:].indirect(offs_t[:]))
        nc.vector.tensor_copy(g_words[:], words[:].indirect(offs_t[:]))

        wps = sb.tile([P, 1], F32, name="wps")
        nc.scalar.mul(wps[:], wp_t[:], 1.2)
        ca_t = ps.tile([P, P], F32, name="ca_t", tag="ca_then_y")
        nc.tensor.transpose(ca_t[:], ca_rows[:], ident[:])
        ca_col = sb.tile([P, BLOCKS], F32, name="ca_col")
        nc.scalar.activation(ca_col[:], ca_t[:, 0:BLOCKS], COPY, scale=0.5)

        fe_tr = ps.tile([P, S], F32, name="fe_tr")
        for t in range(BLOCKS):
            nc.tensor.transpose(fe_tr[:, blk(t)], fe_t[:, blk(t)], ident[:])
        s1 = f32_tile("s1")
        s2 = f32_tile("s2")
        z = f32_tile("z")
        nc.scalar.activation(s1[:], fe_t[:], IDENT, scale=wps[:])
        for t in range(BLOCKS):
            nc.scalar.activation(z[:, blk(t)], fe_tr[:, blk(t)], IDENT, scale=ca_col[:, t : t + 1])
        nc.scalar.activation(s2[:], cur_t[:], COPY, scale=0.84)

        sums = [ps.tile([P, P], F32, name="sum%d" % t) for t in range(BLOCKS)]
        for i, term in enumerate((s1, s2, c)):
            for t in range(BLOCKS):
                nc.tensor.matmul(sums[t][:], term[:, blk(t)], ident[:], start=(i == 0), stop=(i == 2), is_transpose=True)
        fs = f32_tile("fs")
        p_ps = ps.tile([P, S], F32, name="p_ps")
        for t in range(BLOCKS):
            nc.scalar.activation(fs[:, blk(t)], sums[t][:], COPY, scale=-0.25)
        for t in range(BLOCKS):
            nc.tensor.matmul(p_ps[:, blk(t)], z[:, blk(t)], ident[:], start=True, stop=False, is_transpose=True)
            nc.tensor.matmul(p_ps[:, blk(t)], fs[:, blk(t)], ident[:], start=False, stop=True, is_transpose=True)

        w_bf = sb.tile([P, N, 4], BF16, name="w_bf", tag="c_w_d", align_bytes=64)
        nc.scalar.copy(out=w_bf[:], in_=w_raw[:].rearrange("p j n -> p n j"))
        p_sb = sb.tile([P, S], F32, name="p_sb", tag="w_then_p", align_bytes=64)
        nc.scalar.copy(out=p_sb[:], in_=p_ps[:])

        w_codes = sb.tile([P, N], U32, name="w_codes", align_bytes=64)
        w_scales = sb.tile([P, N], U8, name="w_scales", align_bytes=64)
        nc.vector.quantize_mx(
            out=w_codes[:].bitcast(FP8X4),
            scales=w_scales[:],
            in_=w_bf[:].rearrange("p n j -> p (n j)"),
        )
        ys = [ps.tile([P, HALF], F32, name="y0"), ps.tile([P, HALF], F32, name="y1", tag="ca_then_y")]
        for h in range(2):
            nc.tensor.matmul_mx(
                out=ys[h][:],
                lhsT=w_codes[:].bitcast(FP8X4),
                lhsT_scale=w_scales[:],
                rhs=g_words[:, cols(h)].bitcast(FP8X4),
                rhs_scale=g_scales[:, cols(h)],
                start=True,
                stop=True,
            )

        d_t = sb.tile([P, S], F32, name="d", tag="c_w_d", align_bytes=64)
        e_t = f32_tile("e")
        nc.vector.tensor_tensor(d_t[:], fh_t[:], da_t[:], MULT)
        for h in range(2):
            nc.vector.scalar_tensor_tensor(e_t[:, cols(h)], ys[h][:], -0.2, p_sb[:, cols(h)], MULT, ADD)

        r_t = f32_tile("r")
        o_t = f32_tile("o")
        for h in range(2):
            nc.vector.tensor_tensor(r_t[:, cols(h)], e_t[:].indirect(rt_t[:, lcols(h)]), d_t[:, cols(h)], SUB)
        for h in range(2):
            nc.vector.tensor_tensor(o_t[:, cols(h)], e_t[:].indirect(lt_t[:, lcols(h)]), r_t[:, cols(h)], SUB)
            nc.sync.dma_start(out=out[:, cols(h)], in_=o_t[:, cols(h)])
